import numpy as np, ml_dtypes
CORES = [15,47,79,175,207]
N = 5
KB, QP = 2, 256
def setup_inputs(rng):
    q = rng.standard_normal((N, 128, QP), dtype=np.float32) / 4; k = rng.standard_normal((N, 128, KB * 128), dtype=np.float32)
    a = 2 * np.pi * rng.random((N, QP)); s = 400 * rng.random((N, QP)) ** 1.5; q[:, 0, :] = s * np.cos(a); q[:, 1, :] = s * np.sin(a); q[:, 2, :] = 150 * rng.standard_normal((N, QP)); k[:, 2, :] = 1 + k[:, 2, :] / 50
    a = (2 * np.pi * rng.random() + np.pi / 2 * (rng.permutation(N).reshape(N, 1, 1) + 0.5) / N - 0.5 + (np.arange(KB).reshape(1, KB, 1) + rng.random((N, KB, 128))) / KB).reshape(N, KB * 128); k[:, 0, :] = np.cos(a); k[:, 1, :] = np.sin(a)
    return {"q": q.astype(ml_dtypes.bfloat16), "k": k.astype(ml_dtypes.bfloat16), "v": rng.standard_normal((N, 128, KB * 128), dtype=np.float32).astype(ml_dtypes.bfloat16)}
def setup_inputs_big(rng):
    d = setup_inputs(rng)
    for k in ("v",): d[k] = (d[k].astype(np.float32) * 1048576.0).astype(d[k].dtype)
    return d
def setup_inputs_small(rng):
    d = setup_inputs(rng)
    for k in ("v",): d[k] = (d[k].astype(np.float32) * (1 / 1048576.0)).astype(d[k].dtype)
    return d
def reference(q, k, v):
    Q, K, V = q.astype(np.float64), k.astype(np.float64), v.astype(np.float64)
    y = np.zeros((N, QP, 128))
    for r in range(N):
        js = list(range(r + 1))
        S = np.concatenate([K[j].T @ Q[r] for j in js], axis=0)
        kp = np.concatenate([j * KB * 128 + np.arange(KB * 128) for j in js]); S = np.where(kp[:, None] <= (r * QP + np.arange(QP))[None, :], S, -np.inf)
        P = np.exp(S - S.max(axis=0)); P = P / P.sum(axis=0)
        y[r] = P.T @ np.concatenate([V[j][:, 128 * b:128 * b + 128] for j in js for b in range(KB)], axis=0)
    return {"y": y.astype(ml_dtypes.bfloat16)}

@@ -1,0 +1,235 @@
+from concourse.mybir import AluOpType, AxisListType, ActivationFunctionType
+
+N = 5
+NCORES = 256
+RELAY = 0
+NEG = -30000.0
+
+SCRATCH = {
+    "qs": ("sbuf", [128, 256], "bfloat16"),
+    "kall": ("sbuf", [128, 256 * N], "bfloat16"),
+    "vall": ("sbuf", [128, 256 * N], "bfloat16"),
+    "dd": ("sbuf", [128, 260], "float32"),
+    "ident": ("sbuf", [128, 128], "bfloat16"),
+    "mask": ("sbuf", [128, 512], "bfloat16"),
+    "nm": ("sbuf", [128, 16], "float32"),
+    "negM": ("sbuf", [128, 4], "float32"),
+    "afac": ("sbuf", [128, 4], "float32"),
+    "lown": ("sbuf", [128, 4], "float32"),
+    "lc": ("sbuf", [128, 16], "float32"),
+    "lsum": ("sbuf", [128, 4], "float32"),
+    "rl": ("sbuf", [128, 4], "float32"),
+    "P": ("sbuf", [128, 512 * N], "bfloat16"),
+    "PT": ("sbuf", [128, 512 * N], "bfloat16"),
+    "Oa": ("sbuf", [128, 256], "bfloat16"),
+    "ysb": ("sbuf", [128, 256], "bfloat16"),
+    "s0": ("psum", [128, 512], "float32"),
+    "s1": ("psum", [128, 512], "float32"),
+    "s2": ("psum", [128, 512], "float32"),
+    "s3": ("psum", [128, 512], "float32"),
+    "s4": ("psum", [128, 512], "float32"),
+    "o0": ("psum", [128, 512], "float32"),
+    "o1": ("psum", [128, 512], "float32"),
+}
+SEMAPHORES = (["ldk", "ldq", "ldv", "iot", "cst", "sM", "pvo", "sa", "sOa", "sla", "sls", "srl", "so0", "so1", "sy", "st",
+               "sent"]
+              + ["%s%d" % (n, i) for n in ("sS", "sm", "se", "sT", "sc", "karr", "varr") for i in range(N)])
+
+
+def _bits(m):
+    return bin(m).count("1")
+
+
+def _relay_core(j, T, topo):
+    far = list(range(j + 1, N))[RELAY:] if RELAY > 0 else []
+    if not far:
+        return None, []
+    me = T.cores[j]
+    for c in range(NCORES):
+        if (topo.host(c) == topo.host(me) and topo.chip(c) == topo.chip(me) and topo.die(c) != topo.die(me)
+                and T.rank_of(c) is None and all(topo.may_write(c, T.cores[d]) for d in far)):
+            return c, far
+    return None, []
+
+
+def _send(g, core, T, topo, j, dsts, buf, arr):
+    tot = 0
+    ap = T[buf][:, 256 * j:256 * j + 256]
+    for d, m in dsts:
+        rid, pid = topo.addr(d, core)
+        g.remote_dma(out_ap=ap, in_ap=ap, remote_sem=T.sem["%s%d" % (arr, j)], local_sem=T.sem.sent, pid=pid,
+                     routing_id=rid, dma_engine_mask=m)
+        tot += _bits(m)
+    return tot
+
+
+def rank_program(g, core, T, topo):
+    sem = T.sem
+    r = T.rank_of(core)
+    if r is None:
+        for j in range(N):
+            c, far = _relay_core(j, T, topo)
+            if c == core:
+                src = T.cores[j]
+                n_in = _bits(topo.mask(src, core) & ~topo.mask(src, T.cores[far[0]]))
+                dsts = [(T.cores[d], topo.mask(core, T.cores[d])) for d in far]
+                g.wait_ge(sem["karr%d" % j], n_in)
+                tot = _send(g, core, T, topo, j, dsts, "kall", "karr")
+                g.wait_ge(sem["varr%d" % j], n_in)
+                tot += _send(g, core, T, topo, j, dsts, "vall", "varr")
+                g.wait_ge(sem.sent, tot)
+        return
+
+    A, X, F = AluOpType, AxisListType.X, ActivationFunctionType
+    pe, dve, act, sp = g.tensor, g.vector, g.scalar, g.sync
+    nb = r + 1
+    blocks = [r] + list(range(r - 1, -1, -1))
+    S = [T["s%d" % i] for i in range(N)]
+    O = [T.o0, T.o1]
+    so = [sem.so0, sem.so1]
+
+    def ks(j):
+        return T.kall[:, 256 * j:256 * j + 256]
+
+    def vs(j, b):
+        return T.vall[:, 256 * j + 128 * b:256 * j + 128 * b + 128]
+
+    def Pb(i, h, b):
+        return T.P[:, 512 * i + 256 * h + 128 * b:512 * i + 256 * h + 128 * b + 128]
+
+    def col(t, c):
+        return t[:, c:c + 1]
+
+    sp.dma_start(ks(r), T.k[:]).then_inc(sem.ldk, 16)
+    act.dma_start(T.qs[:], T.q[:]).then_inc(sem.ldq, 16)
+    sp.dma_start(T.vall[:, 256 * r:256 * r + 256], T.v[:]).then_inc(sem.ldv, 16)
+
+    g.iota(T.dd[:, 0:257], [[1, 257]], -1, -2, allow_small_or_imprecise_dtypes=True).then_inc(sem.iot, 1)
+    dests = list(range(r + 1, N))
+    if dests:
+        rc, far = _relay_core(r, T, topo)
+        near = [d for d in dests if d not in far]
+        dl = [(T.cores[d], topo.mask(core, T.cores[d])) for d in near]
+        if rc is not None:
+            dl = [(rc, topo.mask(core, rc) & ~topo.mask(core, T.cores[far[0]]))] + dl
+        g.wait_ge(sem.ldk, 16)
+        tot = _send(g, core, T, topo, r, dl, "kall", "karr")
+        g.wait_ge(sem.ldv, 16)
+        tot += _send(g, core, T, topo, r, dl, "vall", "varr")
+        g.wait_ge(sem.sent, tot)
+
+    dve.wait_ge(sem.iot, 1)
+    dve.tensor_scalar(T.ident[:], T.dd[:, 1:257:2], 0.0, None, A.is_equal).then_inc(sem.cst, 1)
+    for h in range(2):
+        dve.tensor_scalar(T.mask[:, 256 * h:256 * h + 256], T.dd[:, 1 - h:257 - h], 0.0, NEG, A.is_gt,
+                          A.mult).then_inc(sem.cst, 1)
+
+    def transposes(i):
+        pe.wait_ge(sem["se%d" % i], 2)
+        for b in range(2):
+            for h in range(2):
+                c = 128 * (2 * b + h)
+                pe.matmul(S[i][:, c:c + 128], Pb(i, h, b), T.ident[:], True, True).then_inc(sem["sT%d" % i], 1)
+
+    def copy_pt(i):
+        dve.wait_ge(sem["sT%d" % i], 4)
+        dve.tensor_copy(T.PT[:, 512 * i:512 * i + 512], S[i][:]).then_inc(sem["sc%d" % i], 1)
+
+    def maxima(i, n):
+        dve.wait_ge(sem["sS%d" % i], n)
+        for h in range(2):
+            dve.tensor_reduce(col(T.nm, 8 * h + i), S[i][:, 256 * h:256 * h + 256], X, A.max,
+                              negate=True).then_inc(sem["sm%d" % i], 1)
+
+    def pt(i, h, b):
+        c = 512 * i + 128 * (2 * b + h)
+        return T.PT[:, c:c + 128]
+
+    pe.wait_ge(sem.ldq, 16)
+    pe.wait_ge(sem.ldk, 16)
+    pe.wait_ge(sem.cst, 3)
+    for h in range(2):
+        out = S[0][:, 256 * h:256 * h + 256]
+        pe.matmul(out, T.qs[:, h:256:2], ks(r), True, False).then_inc(sem.sS0, 1)
+        pe.matmul(out, T.ident[:], T.mask[:, 256 * h:256 * h + 256], False, True).then_inc(sem.sS0, 1)
+    maxima(0, 4)
+    act.wait_ge(sem.sm0, 2)
+    for h in range(2):
+        act.activation(T.P[:, 256 * h:256 * h + 256], S[0][:, 256 * h:256 * h + 256], F.Exp, bias=col(T.nm, 8 * h),
+                       scale=1.0, accum_out=col(T.lown, h)).then_inc(sem.se0, 1)
+    transposes(0)
+    copy_pt(0)
+    pe.wait_ge(sem.sc0, 1)
+    pe.wait_ge(sem.ldv, 16)
+    for h in range(2):
+        for b in range(2):
+            pe.matmul(O[h][:, 0:128], pt(0, h, b), vs(r, b), b == 0, b == 1).then_inc(sem.pvo, 1)
+
+    if nb == 1:
+        dve.wait_ge(sem.se0, 2)
+        dve.reciprocal(T.rl[:, 0:2], T.lown[:, 0:2]).then_inc(sem.srl, 1)
+        done = [(sem.pvo, 4), (sem.pvo, 4)]
+    else:
+        for i in range(1, nb):
+            j = blocks[i]
+            pe.wait_ge(sem["karr%d" % j], _bits(topo.mask(T.cores[j], core)))
+            for h in range(2):
+                pe.matmul(S[i][:, 256 * h:256 * h + 256], T.qs[:, h:256:2], ks(j), True, True).then_inc(sem["sS%d" % i], 1)
+            maxima(i, 2)
+        for i in range(nb):
+            dve.wait_ge(sem["sm%d" % i], 2)
+        for h in range(2):
+            dve.tensor_reduce(col(T.negM, h), T.nm[:, 8 * h:8 * h + nb], X, A.min).then_inc(sem.sM, 1)
+        act.wait_ge(sem.sM, 2)
+        for h in range(2):
+            act.activation(col(T.afac, h), col(T.nm, 8 * h), F.Exp, bias=col(T.negM, h), scale=-1.0).then_inc(sem.sa, 1)
+        for i in range(1, nb):
+            for h in range(2):
+                c = 512 * i + 256 * h
+                act.activation(T.P[:, c:c + 256], S[i][:, 256 * h:256 * h + 256], F.Exp, bias=col(T.negM, h), scale=1.0,
+                               accum_out=col(T.lc, 8 * h + i)).then_inc(sem["se%d" % i], 1)
+        dve.wait_ge(sem.sa, 2)
+        dve.wait_ge(sem.pvo, 4)
+        for h in range(2):
+            dve.tensor_scalar(T.Oa[:, 128 * h:128 * h + 128], O[h][:, 0:128], col(T.afac, h), None,
+                              A.mult).then_inc(sem.sOa, 1)
+        for h in range(2):
+            dve.tensor_scalar(col(T.lc, 8 * h), col(T.lown, h), col(T.afac, h), None, A.mult).then_inc(sem.sla, 1)
+        pe.wait_ge(sem.sOa, 2)
+        for h in range(2):
+            pe.matmul(O[h][:, 0:128], T.ident[:], T.Oa[:, 128 * h:128 * h + 128], True, False).then_inc(so[h], 1)
+
+        def sums():
+            for i in range(1, nb):
+                dve.wait_ge(sem["se%d" % i], 2)
+            dve.wait_ge(sem.sla, 2)
+            for h in range(2):
+                dve.tensor_reduce(col(T.lsum, h), T.lc[:, 8 * h:8 * h + nb], X, A.add).then_inc(sem.sls, 1)
+            dve.wait_ge(sem.sls, 2)
+            dve.reciprocal(T.rl[:, 0:2], T.lsum[:, 0:2]).then_inc(sem.srl, 1)
+
+        transposes(1)
+        for i in range(1, nb):
+            if i == nb - 1:
+                sums()
+            copy_pt(i)
+            if i + 1 < nb:
+                transposes(i + 1)
+            j = blocks[i]
+            pe.wait_ge(sem["sc%d" % i], 1)
+            pe.wait_ge(sem["varr%d" % j], _bits(topo.mask(T.cores[j], core)))
+            for h in range(2):
+                for b in range(2):
+                    pe.matmul(O[h][:, 0:128], pt(i, h, b), vs(j, b), False, i == nb - 1 and b == 1).then_inc(so[h], 1)
+        n = 1 + 2 * (nb - 1)
+        done = [(so[0], n), (so[1], n)]
+
+    dve.wait_ge(sem.srl, 1)
+    dve.wait_ge(done[0][0], done[0][1])
+    dve.tensor_scalar(T.ysb[:, 0:128], O[0][:, 0:128], col(T.rl, 0), None, A.mult).then_inc(sem.sy, 1)
+    act.wait_ge(sem.srl, 1)
+    act.wait_ge(done[1][0], done[1][1])
+    act.activation(T.ysb[:, 128:256], O[1][:, 0:128], F.Copy, scale=col(T.rl, 1)).then_inc(sem.sy, 1)
+    sp.wait_ge(sem.sy, 2)
+    sp.dma_start(T.y[:], T.ysb[:]).then_inc(sem.st, 16)
+    sp.wait_ge(sem.st, 16)

@@ -1,62 +1,52 @@
 from concourse.mybir import AluOpType, AxisListType, ActivationFunctionType
 
 N = 5
-NCORES = 256
-RELAY = 0
 NEG = -30000.0
+STEP = 16.0
+NB = 3
 
 SCRATCH = {
     "qs": ("sbuf", [128, 256], "bfloat16"),
     "kall": ("sbuf", [128, 256 * N], "bfloat16"),
     "vall": ("sbuf", [128, 256 * N], "bfloat16"),
     "dd": ("sbuf", [128, 260], "float32"),
-    "ident": ("sbuf", [128, 128], "bfloat16"),
+    "sq": ("sbuf", [128, 128], "float32"),
+    "identD": ("sbuf", [128, 128], "bfloat16"),
+    "identA": ("sbuf", [128, 128], "bfloat16"),
     "mask": ("sbuf", [128, 512], "bfloat16"),
     "nm": ("sbuf", [128, 16], "float32"),
-    "negM": ("sbuf", [128, 4], "float32"),
-    "afac": ("sbuf", [128, 4], "float32"),
-    "lown": ("sbuf", [128, 4], "float32"),
+    "nc": ("sbuf", [128, 16], "float32"),
     "lc": ("sbuf", [128, 16], "float32"),
     "lsum": ("sbuf", [128, 4], "float32"),
     "rl": ("sbuf", [128, 4], "float32"),
     "P": ("sbuf", [128, 512 * N], "bfloat16"),
     "PT": ("sbuf", [128, 512 * N], "bfloat16"),
-    "Oa": ("sbuf", [128, 256], "bfloat16"),
     "ysb": ("sbuf", [128, 256], "bfloat16"),
     "s0": ("psum", [128, 512], "float32"),
     "s1": ("psum", [128, 512], "float32"),
     "s2": ("psum", [128, 512], "float32"),
-    "s3": ("psum", [128, 512], "float32"),
-    "s4": ("psum", [128, 512], "float32"),
+    "t0": ("psum", [128, 512], "float32"),
+    "t1": ("psum", [128, 512], "float32"),
+    "t2": ("psum", [128, 512], "float32"),
     "o0": ("psum", [128, 512], "float32"),
     "o1": ("psum", [128, 512], "float32"),
 }
-SEMAPHORES = (["ldk", "ldq", "ldv", "iot", "cst", "sM", "pvo", "sa", "sOa", "sla", "sls", "srl", "so0", "so1", "sy", "st",
-               "sent"]
-              + ["%s%d" % (n, i) for n in ("sS", "sm", "se", "sT", "sc", "karr", "varr") for i in range(N)])
+SEMAPHORES = (["ldk", "ldq", "ldv", "iot", "cst", "sqs", "ida", "sls", "srl", "so0", "so1", "sy", "st", "sent"]
+              + ["%s%d" % (n, i) for n in ("sS", "sm", "snx", "sny", "sex", "sey", "sT", "sca", "scb", "karr", "varr")
+                 for i in range(N)])
 
 
 def _bits(m):
     return bin(m).count("1")
 
 
-def _relay_core(j, T, topo):
-    far = list(range(j + 1, N))[RELAY:] if RELAY > 0 else []
-    if not far:
-        return None, []
-    me = T.cores[j]
-    for c in range(NCORES):
-        if (topo.host(c) == topo.host(me) and topo.chip(c) == topo.chip(me) and topo.die(c) != topo.die(me)
-                and T.rank_of(c) is None and all(topo.may_write(c, T.cores[d]) for d in far)):
-            return c, far
-    return None, []
-
-
 def _send(g, core, T, topo, j, dsts, buf, arr):
     tot = 0
     ap = T[buf][:, 256 * j:256 * j + 256]
-    for d, m in dsts:
-        rid, pid = topo.addr(d, core)
+    for d in dsts:
+        c = T.cores[d]
+        m = topo.mask(core, c)
+        rid, pid = topo.addr(c, core)
         g.remote_dma(out_ap=ap, in_ap=ap, remote_sem=T.sem["%s%d" % (arr, j)], local_sem=T.sem.sent, pid=pid,
                      routing_id=rid, dma_engine_mask=m)
         tot += _bits(m)
@@ -67,26 +57,22 @@ def rank_program(g, core, T, topo):
     sem = T.sem
     r = T.rank_of(core)
     if r is None:
-        for j in range(N):
-            c, far = _relay_core(j, T, topo)
-            if c == core:
-                src = T.cores[j]
-                n_in = _bits(topo.mask(src, core) & ~topo.mask(src, T.cores[far[0]]))
-                dsts = [(T.cores[d], topo.mask(core, T.cores[d])) for d in far]
-                g.wait_ge(sem["karr%d" % j], n_in)
-                tot = _send(g, core, T, topo, j, dsts, "kall", "karr")
-                g.wait_ge(sem["varr%d" % j], n_in)
-                tot += _send(g, core, T, topo, j, dsts, "vall", "varr")
-                g.wait_ge(sem.sent, tot)
         return
 
     A, X, F = AluOpType, AxisListType.X, ActivationFunctionType
     pe, dve, act, sp = g.tensor, g.vector, g.scalar, g.sync
     nb = r + 1
     blocks = [r] + list(range(r - 1, -1, -1))
-    S = [T["s%d" % i] for i in range(N)]
+    S = [T["s%d" % i] for i in range(NB)]
+    TP = [T["t%d" % i] for i in range(NB)]
     O = [T.o0, T.o1]
     so = [sem.so0, sem.so1]
+
+    def sn(h, i):
+        return sem["%s%d" % (("snx", "sny")[h], i)]
+
+    def se(h, i):
+        return sem["%s%d" % (("sex", "sey")[h], i)]
 
     def ks(j):
         return T.kall[:, 256 * j:256 * j + 256]
@@ -96,6 +82,10 @@ def rank_program(g, core, T, topo):
 
     def Pb(i, h, b):
         return T.P[:, 512 * i + 256 * h + 128 * b:512 * i + 256 * h + 128 * b + 128]
+
+    def pt(i, h, b):
+        c = 512 * i + 128 * (2 * b + h)
+        return T.PT[:, c:c + 128]
 
     def col(t, c):
         return t[:, c:c + 1]
@@ -107,128 +97,142 @@ def rank_program(g, core, T, topo):
     g.iota(T.dd[:, 0:257], [[1, 257]], -1, -2, allow_small_or_imprecise_dtypes=True).then_inc(sem.iot, 1)
     dests = list(range(r + 1, N))
     if dests:
-        rc, far = _relay_core(r, T, topo)
-        near = [d for d in dests if d not in far]
-        dl = [(T.cores[d], topo.mask(core, T.cores[d])) for d in near]
-        if rc is not None:
-            dl = [(rc, topo.mask(core, rc) & ~topo.mask(core, T.cores[far[0]]))] + dl
         g.wait_ge(sem.ldk, 16)
-        tot = _send(g, core, T, topo, r, dl, "kall", "karr")
+        tot = _send(g, core, T, topo, r, dests, "kall", "karr")
         g.wait_ge(sem.ldv, 16)
-        tot += _send(g, core, T, topo, r, dl, "vall", "varr")
+        tot += _send(g, core, T, topo, r, dests[::-1], "vall", "varr")
         g.wait_ge(sem.sent, tot)
 
     dve.wait_ge(sem.iot, 1)
-    dve.tensor_scalar(T.ident[:], T.dd[:, 1:257:2], 0.0, None, A.is_equal).then_inc(sem.cst, 1)
+    dve.tensor_scalar(T.identD[:], T.dd[:, 1:257:2], 0.0, None, A.is_equal).then_inc(sem.cst, 1)
     for h in range(2):
         dve.tensor_scalar(T.mask[:, 256 * h:256 * h + 256], T.dd[:, 1 - h:257 - h], 0.0, NEG, A.is_gt,
                           A.mult).then_inc(sem.cst, 1)
+    act.wait_ge(sem.iot, 1)
+    act.activation(T.sq[:], T.dd[:, 1:257:2], F.Square).then_inc(sem.sqs, 1)
+    act.wait_ge(sem.sqs, 1)
+    act.activation(T.identA[:], T.sq[:], F.Exp, scale=-100.0).then_inc(sem.ida, 1)
+
+    def scores(i):
+        bank = S[i % NB]
+        if i >= NB:
+            pe.wait_ge(sem["sm%d" % (i - NB)], 2)
+            pe.wait_ge(se(0, i - NB), 1)
+            pe.wait_ge(se(1, i - NB), 1)
+        j = blocks[i]
+        if i == 0:
+            pe.wait_ge(sem.ldq, 16)
+            pe.wait_ge(sem.ldk, 16)
+            pe.wait_ge(sem.cst, 3)
+        else:
+            pe.wait_ge(sem["karr%d" % j], _bits(topo.mask(T.cores[j], core)))
+        for h in range(2):
+            out = bank[:, 256 * h:256 * h + 256]
+            pe.matmul(out, T.qs[:, h:256:2], ks(j), True, i != 0).then_inc(sem["sS%d" % i], 1)
+            if i == 0:
+                pe.matmul(out, T.identD[:], T.mask[:, 256 * h:256 * h + 256], False, True).then_inc(sem.sS0, 1)
+
+    def shift(i):
+        bank = S[i % NB]
+        off = ((nb - 1) / 2.0 - i) * STEP
+        dve.wait_ge(sem["sS%d" % i], 4 if i == 0 else 2)
+        for h in range(2):
+            dve.tensor_reduce(col(T.nm, 8 * h + i), bank[:, 256 * h:256 * h + 256], X, A.max,
+                              negate=True).then_inc(sem["sm%d" % i], 1)
+        dve.wait_ge(sem["sm%d" % i], 2)
+        for h in range(2):
+            if i == 0:
+                dve.tensor_scalar(col(T.nc, 8 * h), col(T.nm, 8 * h), -off, None, A.add).then_inc(sn(h, 0), 1)
+            else:
+                dve.wait_ge(sn(h, i - 1), 1)
+                dve.tensor_scalar(col(T.nc, 8 * h + i), col(T.nm, 8 * h + i), -off, col(T.nc, 8 * h + i - 1), A.add,
+                                  A.min).then_inc(sn(h, i), 1)
+
+    def weights(i):
+        bank = S[i % NB]
+        for h in range(2):
+            c = 512 * i + 256 * h
+            act.wait_ge(sn(h, i), 1)
+            act.activation(T.P[:, c:c + 256], bank[:, 256 * h:256 * h + 256], F.Exp, bias=col(T.nc, 8 * h + i), scale=1.0,
+                           accum_out=col(T.lc, 8 * h + i)).then_inc(se(h, i), 1)
 
     def transposes(i):
-        pe.wait_ge(sem["se%d" % i], 2)
-        for b in range(2):
-            for h in range(2):
+        bank = TP[i % NB]
+        if i == 0:
+            pe.wait_ge(sem.ida, 1)
+        if i >= NB:
+            pe.wait_ge(sem["sca%d" % (i - NB)], 1)
+            pe.wait_ge(sem["scb%d" % (i - NB)], 1)
+        for h in range(2):
+            pe.wait_ge(se(h, i), 1)
+            for b in range(2):
                 c = 128 * (2 * b + h)
-                pe.matmul(S[i][:, c:c + 128], Pb(i, h, b), T.ident[:], True, True).then_inc(sem["sT%d" % i], 1)
+                pe.matmul(bank[:, c:c + 128], Pb(i, h, b), T.identA[:], True, True).then_inc(sem["sT%d" % i], 1)
 
     def copy_pt(i):
+        bank = TP[i % NB]
         dve.wait_ge(sem["sT%d" % i], 4)
-        dve.tensor_copy(T.PT[:, 512 * i:512 * i + 512], S[i][:]).then_inc(sem["sc%d" % i], 1)
+        dve.tensor_copy(T.PT[:, 512 * i:512 * i + 256], bank[:, 0:256]).then_inc(sem["sca%d" % i], 1)
+        dve.tensor_copy(T.PT[:, 512 * i + 256:512 * i + 512], bank[:, 256:512]).then_inc(sem["scb%d" % i], 1)
 
-    def maxima(i, n):
-        dve.wait_ge(sem["sS%d" % i], n)
-        for h in range(2):
-            dve.tensor_reduce(col(T.nm, 8 * h + i), S[i][:, 256 * h:256 * h + 256], X, A.max,
-                              negate=True).then_inc(sem["sm%d" % i], 1)
-
-    def pt(i, h, b):
-        c = 512 * i + 128 * (2 * b + h)
-        return T.PT[:, c:c + 128]
-
-    pe.wait_ge(sem.ldq, 16)
-    pe.wait_ge(sem.ldk, 16)
-    pe.wait_ge(sem.cst, 3)
-    for h in range(2):
-        out = S[0][:, 256 * h:256 * h + 256]
-        pe.matmul(out, T.qs[:, h:256:2], ks(r), True, False).then_inc(sem.sS0, 1)
-        pe.matmul(out, T.ident[:], T.mask[:, 256 * h:256 * h + 256], False, True).then_inc(sem.sS0, 1)
-    maxima(0, 4)
-    act.wait_ge(sem.sm0, 2)
-    for h in range(2):
-        act.activation(T.P[:, 256 * h:256 * h + 256], S[0][:, 256 * h:256 * h + 256], F.Exp, bias=col(T.nm, 8 * h),
-                       scale=1.0, accum_out=col(T.lown, h)).then_inc(sem.se0, 1)
-    transposes(0)
-    copy_pt(0)
-    pe.wait_ge(sem.sc0, 1)
-    pe.wait_ge(sem.ldv, 16)
-    for h in range(2):
-        for b in range(2):
-            pe.matmul(O[h][:, 0:128], pt(0, h, b), vs(r, b), b == 0, b == 1).then_inc(sem.pvo, 1)
-
-    if nb == 1:
-        dve.wait_ge(sem.se0, 2)
-        dve.reciprocal(T.rl[:, 0:2], T.lown[:, 0:2]).then_inc(sem.srl, 1)
-        done = [(sem.pvo, 4), (sem.pvo, 4)]
-    else:
-        for i in range(1, nb):
-            j = blocks[i]
-            pe.wait_ge(sem["karr%d" % j], _bits(topo.mask(T.cores[j], core)))
-            for h in range(2):
-                pe.matmul(S[i][:, 256 * h:256 * h + 256], T.qs[:, h:256:2], ks(j), True, True).then_inc(sem["sS%d" % i], 1)
-            maxima(i, 2)
-        for i in range(nb):
-            dve.wait_ge(sem["sm%d" % i], 2)
-        for h in range(2):
-            dve.tensor_reduce(col(T.negM, h), T.nm[:, 8 * h:8 * h + nb], X, A.min).then_inc(sem.sM, 1)
-        act.wait_ge(sem.sM, 2)
-        for h in range(2):
-            act.activation(col(T.afac, h), col(T.nm, 8 * h), F.Exp, bias=col(T.negM, h), scale=-1.0).then_inc(sem.sa, 1)
-        for i in range(1, nb):
-            for h in range(2):
-                c = 512 * i + 256 * h
-                act.activation(T.P[:, c:c + 256], S[i][:, 256 * h:256 * h + 256], F.Exp, bias=col(T.negM, h), scale=1.0,
-                               accum_out=col(T.lc, 8 * h + i)).then_inc(sem["se%d" % i], 1)
-        dve.wait_ge(sem.sa, 2)
-        dve.wait_ge(sem.pvo, 4)
-        for h in range(2):
-            dve.tensor_scalar(T.Oa[:, 128 * h:128 * h + 128], O[h][:, 0:128], col(T.afac, h), None,
-                              A.mult).then_inc(sem.sOa, 1)
-        for h in range(2):
-            dve.tensor_scalar(col(T.lc, 8 * h), col(T.lown, h), col(T.afac, h), None, A.mult).then_inc(sem.sla, 1)
-        pe.wait_ge(sem.sOa, 2)
-        for h in range(2):
-            pe.matmul(O[h][:, 0:128], T.ident[:], T.Oa[:, 128 * h:128 * h + 128], True, False).then_inc(so[h], 1)
-
-        def sums():
-            for i in range(1, nb):
-                dve.wait_ge(sem["se%d" % i], 2)
-            dve.wait_ge(sem.sla, 2)
-            for h in range(2):
-                dve.tensor_reduce(col(T.lsum, h), T.lc[:, 8 * h:8 * h + nb], X, A.add).then_inc(sem.sls, 1)
-            dve.wait_ge(sem.sls, 2)
-            dve.reciprocal(T.rl[:, 0:2], T.lsum[:, 0:2]).then_inc(sem.srl, 1)
-
-        transposes(1)
-        for i in range(1, nb):
-            if i == nb - 1:
-                sums()
-            copy_pt(i)
-            if i + 1 < nb:
-                transposes(i + 1)
-            j = blocks[i]
-            pe.wait_ge(sem["sc%d" % i], 1)
+    def products(i):
+        j = blocks[i]
+        if i == 0:
+            pe.wait_ge(sem.ldv, 16)
+        else:
             pe.wait_ge(sem["varr%d" % j], _bits(topo.mask(T.cores[j], core)))
+        for b in range(2):
+            pe.wait_ge(sem["%s%d" % (("sca", "scb")[b], i)], 1)
             for h in range(2):
-                for b in range(2):
-                    pe.matmul(O[h][:, 0:128], pt(i, h, b), vs(j, b), False, i == nb - 1 and b == 1).then_inc(so[h], 1)
-        n = 1 + 2 * (nb - 1)
-        done = [(so[0], n), (so[1], n)]
+                pe.matmul(O[h][:, 0:128], pt(i, h, b), vs(j, b), i == 0 and b == 0,
+                          i == nb - 1 and b == 1).then_inc(so[h], 1)
 
-    dve.wait_ge(sem.srl, 1)
-    dve.wait_ge(done[0][0], done[0][1])
+    def sums():
+        for i in range(nb):
+            for h in range(2):
+                dve.wait_ge(se(h, i), 1)
+        if nb == 1:
+            for h in range(2):
+                dve.reciprocal(col(T.rl, h), col(T.lc, 8 * h)).then_inc(sem.srl, 1)
+            return 2
+        for h in range(2):
+            dve.tensor_reduce(col(T.lsum, h), T.lc[:, 8 * h:8 * h + nb], X, A.add).then_inc(sem.sls, 1)
+        dve.wait_ge(sem.sls, 2)
+        dve.reciprocal(T.rl[:, 0:2], T.lsum[:, 0:2]).then_inc(sem.srl, 1)
+        return 1
+
+    for i in range(nb):
+        weights(i)
+
+    nrl = 1
+    scores(0)
+    shift(0)
+    transposes(0)
+    if nb == 1:
+        nrl = sums()
+    copy_pt(0)
+    products(0)
+    if nb > 1:
+        scores(1)
+        shift(1)
+        for i in range(1, nb):
+            if i + 1 < nb:
+                scores(i + 1)
+                shift(i + 1)
+            transposes(i)
+            if i == nb - 1:
+                nrl = sums()
+            copy_pt(i)
+            if i > 1:
+                products(i - 1)
+        products(nb - 1)
+
+    n = 2 * nb
+    dve.wait_ge(sem.srl, nrl)
+    dve.wait_ge(so[0], n)
     dve.tensor_scalar(T.ysb[:, 0:128], O[0][:, 0:128], col(T.rl, 0), None, A.mult).then_inc(sem.sy, 1)
-    act.wait_ge(sem.srl, 1)
-    act.wait_ge(done[1][0], done[1][1])
+    act.wait_ge(sem.srl, nrl)
+    act.wait_ge(so[1], n)
     act.activation(T.ysb[:, 128:256], O[1][:, 0:128], F.Copy, scale=col(T.rl, 1)).then_inc(sem.sy, 1)
     sp.wait_ge(sem.sy, 2)
     sp.dma_start(T.y[:], T.ysb[:]).then_inc(sem.st, 16)

from concourse.mybir import AluOpType, AxisListType, ActivationFunctionType

N = 5
NEG = -30000.0
STEP = 16.0
NB = 3

SCRATCH = {
    "qs": ("sbuf", [128, 256], "bfloat16"),
    "kall": ("sbuf", [128, 256 * N], "bfloat16"),
    "vall": ("sbuf", [128, 256 * N], "bfloat16"),
    "dd": ("sbuf", [128, 260], "float32"),
    "sq": ("sbuf", [128, 128], "float32"),
    "identD": ("sbuf", [128, 128], "bfloat16"),
    "identA": ("sbuf", [128, 128], "bfloat16"),
    "mask": ("sbuf", [128, 512], "bfloat16"),
    "nm": ("sbuf", [128, 16], "float32"),
    "nc": ("sbuf", [128, 16], "float32"),
    "lc": ("sbuf", [128, 16], "float32"),
    "lsum": ("sbuf", [128, 4], "float32"),
    "rl": ("sbuf", [128, 4], "float32"),
    "P": ("sbuf", [128, 512 * N], "bfloat16"),
    "PT": ("sbuf", [128, 512 * N], "bfloat16"),
    "ysb": ("sbuf", [128, 256], "bfloat16"),
    "s0": ("psum", [128, 512], "float32"),
    "s1": ("psum", [128, 512], "float32"),
    "s2": ("psum", [128, 512], "float32"),
    "t0": ("psum", [128, 512], "float32"),
    "t1": ("psum", [128, 512], "float32"),
    "t2": ("psum", [128, 512], "float32"),
    "o0": ("psum", [128, 512], "float32"),
    "o1": ("psum", [128, 512], "float32"),
}
SEMAPHORES = (["ldk", "ldq", "ldv", "iot", "cst", "sqs", "ida", "sls", "srl", "so0", "so1", "sy", "st", "sent"]
              + ["%s%d" % (n, i) for n in ("sS", "sm", "snx", "sny", "sex", "sey", "sT", "sca", "scb", "karr", "varr")
                 for i in range(N)])


def _bits(m):
    return bin(m).count("1")


def _send(g, core, T, topo, j, dsts, buf, arr):
    tot = 0
    ap = T[buf][:, 256 * j:256 * j + 256]
    for d in dsts:
        c = T.cores[d]
        m = topo.mask(core, c)
        rid, pid = topo.addr(c, core)
        g.remote_dma(out_ap=ap, in_ap=ap, remote_sem=T.sem["%s%d" % (arr, j)], local_sem=T.sem.sent, pid=pid,
                     routing_id=rid, dma_engine_mask=m)
        tot += _bits(m)
    return tot


def rank_program(g, core, T, topo):
    sem = T.sem
    r = T.rank_of(core)
    if r is None:
        return

    A, X, F = AluOpType, AxisListType.X, ActivationFunctionType
    pe, dve, act, sp = g.tensor, g.vector, g.scalar, g.sync
    nb = r + 1
    blocks = [r] + list(range(r - 1, -1, -1))
    S = [T["s%d" % i] for i in range(NB)]
    TP = [T["t%d" % i] for i in range(NB)]
    O = [T.o0, T.o1]
    so = [sem.so0, sem.so1]

    def sn(h, i):
        return sem["%s%d" % (("snx", "sny")[h], i)]

    def se(h, i):
        return sem["%s%d" % (("sex", "sey")[h], i)]

    def ks(j):
        return T.kall[:, 256 * j:256 * j + 256]

    def vs(j, b):
        return T.vall[:, 256 * j + 128 * b:256 * j + 128 * b + 128]

    def Pb(i, h, b):
        return T.P[:, 512 * i + 256 * h + 128 * b:512 * i + 256 * h + 128 * b + 128]

    def pt(i, h, b):
        c = 512 * i + 128 * (2 * b + h)
        return T.PT[:, c:c + 128]

    def col(t, c):
        return t[:, c:c + 1]

    sp.dma_start(ks(r), T.k[:]).then_inc(sem.ldk, 16)
    act.dma_start(T.qs[:], T.q[:]).then_inc(sem.ldq, 16)
    sp.dma_start(T.vall[:, 256 * r:256 * r + 256], T.v[:]).then_inc(sem.ldv, 16)

    g.iota(T.dd[:, 0:257], [[1, 257]], -1, -2, allow_small_or_imprecise_dtypes=True).then_inc(sem.iot, 1)
    dests = list(range(r + 1, N))
    if dests:
        g.wait_ge(sem.ldk, 16)
        tot = _send(g, core, T, topo, r, dests, "kall", "karr")
        g.wait_ge(sem.ldv, 16)
        tot += _send(g, core, T, topo, r, dests[::-1], "vall", "varr")
        g.wait_ge(sem.sent, tot)

    dve.wait_ge(sem.iot, 1)
    dve.tensor_scalar(T.identD[:], T.dd[:, 1:257:2], 0.0, None, A.is_equal).then_inc(sem.cst, 1)
    for h in range(2):
        dve.tensor_scalar(T.mask[:, 256 * h:256 * h + 256], T.dd[:, 1 - h:257 - h], 0.0, NEG, A.is_gt,
                          A.mult).then_inc(sem.cst, 1)
    act.wait_ge(sem.iot, 1)
    act.activation(T.sq[:], T.dd[:, 1:257:2], F.Square).then_inc(sem.sqs, 1)
    act.wait_ge(sem.sqs, 1)
    act.activation(T.identA[:], T.sq[:], F.Exp, scale=-100.0).then_inc(sem.ida, 1)

    def scores(i):
        bank = S[i % NB]
        if i >= NB:
            pe.wait_ge(sem["sm%d" % (i - NB)], 2)
            pe.wait_ge(se(0, i - NB), 1)
            pe.wait_ge(se(1, i - NB), 1)
        j = blocks[i]
        if i == 0:
            pe.wait_ge(sem.ldq, 16)
            pe.wait_ge(sem.ldk, 16)
            pe.wait_ge(sem.cst, 3)
        else:
            pe.wait_ge(sem["karr%d" % j], _bits(topo.mask(T.cores[j], core)))
        for h in range(2):
            out = bank[:, 256 * h:256 * h + 256]
            pe.matmul(out, T.qs[:, h:256:2], ks(j), True, i != 0).then_inc(sem["sS%d" % i], 1)
            if i == 0:
                pe.matmul(out, T.identD[:], T.mask[:, 256 * h:256 * h + 256], False, True).then_inc(sem.sS0, 1)

    def shift(i):
        bank = S[i % NB]
        off = ((nb - 1) / 2.0 - i) * STEP
        dve.wait_ge(sem["sS%d" % i], 4 if i == 0 else 2)
        for h in range(2):
            dve.tensor_reduce(col(T.nm, 8 * h + i), bank[:, 256 * h:256 * h + 256], X, A.max,
                              negate=True).then_inc(sem["sm%d" % i], 1)
        dve.wait_ge(sem["sm%d" % i], 2)
        for h in range(2):
            if i == 0:
                dve.tensor_scalar(col(T.nc, 8 * h), col(T.nm, 8 * h), -off, None, A.add).then_inc(sn(h, 0), 1)
            else:
                dve.wait_ge(sn(h, i - 1), 1)
                dve.tensor_scalar(col(T.nc, 8 * h + i), col(T.nm, 8 * h + i), -off, col(T.nc, 8 * h + i - 1), A.add,
                                  A.min).then_inc(sn(h, i), 1)

    def weights(i):
        bank = S[i % NB]
        for h in range(2):
            c = 512 * i + 256 * h
            act.wait_ge(sn(h, i), 1)
            act.activation(T.P[:, c:c + 256], bank[:, 256 * h:256 * h + 256], F.Exp, bias=col(T.nc, 8 * h + i), scale=1.0,
                           accum_out=col(T.lc, 8 * h + i)).then_inc(se(h, i), 1)

    def transposes(i):
        bank = TP[i % NB]
        if i == 0:
            pe.wait_ge(sem.ida, 1)
        if i >= NB:
            pe.wait_ge(sem["sca%d" % (i - NB)], 1)
            pe.wait_ge(sem["scb%d" % (i - NB)], 1)
        for h in range(2):
            pe.wait_ge(se(h, i), 1)
            for b in range(2):
                c = 128 * (2 * b + h)
                pe.matmul(bank[:, c:c + 128], Pb(i, h, b), T.identA[:], True, True).then_inc(sem["sT%d" % i], 1)

    def copy_pt(i):
        bank = TP[i % NB]
        dve.wait_ge(sem["sT%d" % i], 4)
        dve.tensor_copy(T.PT[:, 512 * i:512 * i + 256], bank[:, 0:256]).then_inc(sem["sca%d" % i], 1)
        dve.tensor_copy(T.PT[:, 512 * i + 256:512 * i + 512], bank[:, 256:512]).then_inc(sem["scb%d" % i], 1)

    def products(i):
        j = blocks[i]
        if i == 0:
            pe.wait_ge(sem.ldv, 16)
        else:
            pe.wait_ge(sem["varr%d" % j], _bits(topo.mask(T.cores[j], core)))
        for b in range(2):
            pe.wait_ge(sem["%s%d" % (("sca", "scb")[b], i)], 1)
            for h in range(2):
                pe.matmul(O[h][:, 0:128], pt(i, h, b), vs(j, b), i == 0 and b == 0,
                          i == nb - 1 and b == 1).then_inc(so[h], 1)

    def sums():
        for i in range(nb):
            for h in range(2):
                dve.wait_ge(se(h, i), 1)
        if nb == 1:
            for h in range(2):
                dve.reciprocal(col(T.rl, h), col(T.lc, 8 * h)).then_inc(sem.srl, 1)
            return 2
        for h in range(2):
            dve.tensor_reduce(col(T.lsum, h), T.lc[:, 8 * h:8 * h + nb], X, A.add).then_inc(sem.sls, 1)
        dve.wait_ge(sem.sls, 2)
        dve.reciprocal(T.rl[:, 0:2], T.lsum[:, 0:2]).then_inc(sem.srl, 1)
        return 1

    for i in range(nb):
        weights(i)

    nrl = 1
    scores(0)
    shift(0)
    transposes(0)
    if nb == 1:
        nrl = sums()
    copy_pt(0)
    products(0)
    if nb > 1:
        scores(1)
        shift(1)
        for i in range(1, nb):
            if i + 1 < nb:
                scores(i + 1)
                shift(i + 1)
            transposes(i)
            if i == nb - 1:
                nrl = sums()
            copy_pt(i)
            if i > 1:
                products(i - 1)
        products(nb - 1)

    n = 2 * nb
    dve.wait_ge(sem.srl, nrl)
    dve.wait_ge(so[0], n)
    dve.tensor_scalar(T.ysb[:, 0:128], O[0][:, 0:128], col(T.rl, 0), None, A.mult).then_inc(sem.sy, 1)
    act.wait_ge(sem.srl, nrl)
    act.wait_ge(so[1], n)
    act.activation(T.ysb[:, 128:256], O[1][:, 0:128], F.Copy, scale=col(T.rl, 1)).then_inc(sem.sy, 1)
    sp.wait_ge(sem.sy, 2)
    sp.dma_start(T.y[:], T.ysb[:]).then_inc(sem.st, 16)
    sp.wait_ge(sem.st, 16)
